import numpy as np
import ml_dtypes


def mxq(x, axis, fmt="e4m3"):
    dtype, down = {"e4m3": (ml_dtypes.float8_e4m3fn, 7), "e5m2": (ml_dtypes.float8_e5m2, 14)}[fmt]
    v = np.moveaxis(np.asarray(x, np.float32).astype(ml_dtypes.bfloat16).astype(np.float64), axis, -1)
    blocks = v.reshape(v.shape[:-1] + (-1, 32))
    amax = np.abs(blocks).max(-1, keepdims=True)
    byte = np.maximum(np.where(amax > 0, np.frexp(amax)[1] - 1 + 127, 0) - down, 1)
    scale = np.exp2(byte - 127.0)
    codes = (blocks / scale).astype(np.float32).astype(dtype).astype(np.float64)
    return np.moveaxis((codes * scale).reshape(v.shape), -1, axis)


WIDE = False


def mx_kscale(k):
    if not WIDE:
        return np.ones(k)
    levels = np.array([10, -10, 5, -5, 0])
    if k % 512:
        return np.exp2(np.random.permutation(np.resize(levels, k // 32))).repeat(32)
    a = np.empty((k // 512, 16))
    for p in range(k // 512):
        a[p, :8] = np.random.permutation(np.resize(levels, 8))
        for g in range(8):
            far = levels[np.abs(levels - a[p, g]) >= 10]
            a[p, g + 8] = far[np.random.randint(len(far))]
    return np.exp2(a.ravel()).repeat(32)


def f64(x):
    return np.asarray(x).astype(np.float64)


def striped(idx):
    return np.tile(idx.reshape(-1, 16).T, (8, 1)).astype(np.uint16)


def unstriped(offs):
    return offs[:16].T.reshape(-1).astype(np.int64)


E2M1 = np.array([0.0, 0.5, 1.0, 1.5, 2.0, 3.0, 4.0, 6.0, -0.0, -0.5, -1.0, -1.5, -2.0, -3.0, -4.0, -6.0])


def pack_weight(w, fmt):
    k, n = w.shape
    w = f64(np.asarray(w, np.float32).astype(ml_dtypes.bfloat16)).reshape(k // 32, 32, n)
    amax = np.abs(w).max(1)
    if fmt == "e4m3":
        byte = np.frexp(amax)[1] - 1 + 127 - 7
    else:
        mant, ex = np.frexp(amax / 6.0)
        byte = np.where(mant > 0.5, ex, ex - 1) + 127
    byte = np.clip(np.where(amax > 0, byte, 1), 1, 254)
    scaled = (w * np.exp2(127.0 - byte)[:, None, :]).reshape(k, n).astype(np.float32)
    by_word = np.ascontiguousarray(scaled.reshape(k // 512, 128, 4, n).transpose(0, 1, 3, 2))
    if fmt == "e4m3":
        words = by_word.astype(ml_dtypes.float8_e4m3fn).view(np.uint8)
    else:
        c = by_word.astype(ml_dtypes.float4_e2m1fn).view(np.uint8) & 0xF
        words = (c[..., 0::2] | (c[..., 1::2] << 4)).reshape(k // 512, 128, 2 * n)
    return np.ascontiguousarray(words), np.ascontiguousarray(byte.astype(np.uint8).reshape(k // 512, 16, n))


def unpack_weight(words, scales, fmt):
    g, _, n = scales.shape
    words = np.ascontiguousarray(words).reshape(g, 128, n, -1)
    if fmt == "e4m3":
        vals = words.view(ml_dtypes.float8_e4m3fn).astype(np.float64)
    else:
        nib = np.empty((g, 128, n, 4), np.uint8)
        nib[..., 0::2] = words & 0xF
        nib[..., 1::2] = words >> 4
        vals = E2M1[nib]
    vals = vals * np.repeat(np.exp2(scales.astype(np.float64) - 127.0), 8, axis=1)[..., None]
    return vals.transpose(0, 1, 3, 2).reshape(g * 512, n)


def planes(y):
    n, m = y.shape
    v = y.astype(np.float32).astype(ml_dtypes.bfloat16).astype(np.float64).reshape(n // 32, 32, m)
    top = np.abs(v).max(1)
    byte = np.clip(np.where(top > 0, np.frexp(top)[1] - 1 + 127 - 7, 1), 1, 254)
    codes = (v * np.exp2(127.0 - byte)[:, None, :]).reshape(n, m).astype(np.float32).astype(ml_dtypes.float8_e4m3fn).view(np.uint8)
    words = codes.reshape(n // 512, 128, 4, m).transpose(0, 1, 3, 2)
    return np.ascontiguousarray(words), np.ascontiguousarray(byte.astype(np.uint8).reshape(n // 512, 16, m))


def silu(v):
    return v / (1.0 + np.exp(-np.maximum(v, -700.0)))


K, T, E, C, H, TOP, COPIES = 512, 640, 6, 128, 512, 2, 320
PAD = 64


def by_expert(wq, xq):
    return np.concatenate([wq[e].T @ xq[:, e * C:(e + 1) * C] for e in range(E)], axis=1)


def setup_inputs():
    n = np.random.standard_normal
    s = mx_kscale(K)
    u = mx_kscale(H)
    left = TOP * T - E * C - COPIES
    deal = np.repeat(np.arange(E + 2), [C] * E + [COPIES, left]).reshape(TOP, T)[:, np.random.permutation(T)]
    deal = np.take_along_axis(deal, np.argsort(np.random.rand(TOP, T), axis=0), axis=0)
    for _ in range(8):
        s_, t_ = np.random.permutation(T).reshape(2, -1); r = np.random.randint(TOP, size=T // 2); x, y = deal[r, s_].copy(), deal[r, t_].copy()
        ok = ~((deal[:, s_] == y).any(0) | (deal[:, t_] == x).any(0)); deal[r[ok], s_[ok]] = y[ok]; deal[r[ok], t_[ok]] = x[ok]
    order = np.lexsort((np.random.rand(TOP * T), deal.reshape(-1)))[:E * C]
    slot_token = order % T
    pos = np.where(deal == E, E * C + np.arange(T), E * C + T + np.arange(T) % PAD).reshape(-1); pos[order] = np.arange(E * C); pos = pos.reshape(TOP, T)
    g = np.random.uniform(0.5, 1.5, (TOP, T)); g = g / g.sum(0)
    xf = n((K, T))
    x = pack_weight(xf * s[:, None], "e4m3")
    w1 = [pack_weight(m, "e4m3") for m in n((E, K, H)) / np.sqrt(K) / s[None, :, None] * u]
    w2 = [pack_weight(m, "e4m3") for m in n((E, H, K)) / np.sqrt(H) / u[None, :, None]]
    return {
        "x_words": x[0],
        "x_scales": x[1],
        "xr": (xf).astype(np.float32),
        "w1_words": np.stack([m[0] for m in w1]),
        "w1_scales": np.stack([m[1] for m in w1]),
        "w2_words": np.stack([m[0] for m in w2]),
        "w2_scales": np.stack([m[1] for m in w2]),
        "gate": np.stack([np.tile(r, (128, 1)) for r in g]).astype(np.float32),
        "offs": striped(slot_token),
        "pos1": striped(pos[0]),
        "pos2": striped(pos[1]),
    }


def reference(x_words, x_scales, xr, w1_words, w1_scales, w2_words, w2_scales, gate, offs, pos1, pos2):
    w1 = np.stack([unpack_weight(w1_words[e], w1_scales[e], "e4m3") for e in range(E)])
    w2 = np.stack([unpack_weight(w2_words[e], w2_scales[e], "e4m3") for e in range(E)])
    idx = unstriped(offs)
    xq = unpack_weight(x_words, x_scales, "e4m3")[:, idx]
    h = silu(by_expert(w1, xq))
    y = by_expert(w2, mxq(h, 0, "e4m3"))
    y = np.concatenate([y, f64(xr), np.zeros((K, PAD))], axis=1)
    out = sum(f64(gate[r, :1]) * y[:, unstriped(p)] for r, p in enumerate((pos1, pos2)))
    out_0 = out
    return (out_0,) + planes(out_0)

@@ -1,0 +1,221 @@
+from contextlib import ExitStack
+
+import concourse.mybir as mybir
+from concourse.masks import make_identity
+
+K, T, E, C, H, PAD = 512, 640, 6, 128, 512, 64
+S = E * C
+W = S + T + PAD
+FLOPS = 2 * 2 * S * K * H
+
+F32 = mybir.dt.float32
+BF16 = mybir.dt.bfloat16
+I32 = mybir.dt.int32
+U32 = mybir.dt.uint32
+U16 = mybir.dt.uint16
+U8 = mybir.dt.uint8
+FP8X4 = mybir.dt.float8_e4m3fn_x4
+MULT = mybir.AluOpType.mult
+ADD = mybir.AluOpType.add
+SILU = mybir.ActivationFunctionType.Silu
+P = 128
+
+
+def tile_moe_cpy_mlp_silu_kernel(
+    tc, x_words, x_scales, xr, w1_words, w1_scales, w2_words, w2_scales, gate, offs, pos1, pos2, out_0, out_1, out_2
+):
+    nc = tc.nc
+    with ExitStack() as ctx:
+        lists = ctx.enter_context(tc.tile_pool(name="lists", bufs=1))
+        keep = ctx.enter_context(tc.tile_pool(name="keep", bufs=1))
+        ring = ctx.enter_context(tc.tile_pool(name="ring", bufs=3))
+        psum = ctx.enter_context(tc.psum_pool(name="psum", bufs=3))
+        banks = ctx.enter_context(tc.psum_pool(name="banks", bufs=1))
+
+        offs_t = lists.tile([P, S // 16], U16, name="offs_t")
+        pos1_t = lists.tile([P, T // 16], U16, name="pos1_t")
+        pos2_t = lists.tile([P, T // 16], U16, name="pos2_t")
+
+        xw = keep.tile([P, T], U32, name="xw", align_bytes=64)
+        xs = keep.tile([P, T], U8, name="xs", align_bytes=64)
+        w1 = [keep.tile([P, 2, H], U32, name="w1_%d" % j, align_bytes=64) for j in range(3)]
+        w1s = keep.tile([P, E, H], U8, name="w1s", align_bytes=64)
+        w2raw = [keep.tile([P, 2, K], U32, name="w2raw_%d" % j, align_bytes=64) for j in range(3)]
+        w2 = [keep.tile([P, 2, K], U32, name="w2_%d" % j, align_bytes=64) for j in range(3)]
+        w2sraw = [keep.tile([P, K], U8, name="w2sraw_%d" % g, align_bytes=64) for g in range(2)]
+        w2s = [keep.tile([P, K], U8, name="w2s_%d" % g, align_bytes=64) for g in range(2)]
+        y = [keep.tile([P, W], F32, name="y_%d" % t, align_bytes=64) for t in range(4)]
+        g1 = keep.tile([P, T], F32, name="g1", align_bytes=64)
+        g2 = keep.tile([P, T], F32, name="g2", align_bytes=64)
+        ident = keep.tile([P, P], F32, name="ident", align_bytes=64)
+        xg = [keep.tile([P, 2 * C], U32, name="xg_%d" % j, align_bytes=64) for j in range(3)]
+        xgs = [keep.tile([P, 2 * C], U8, name="xgs_%d" % j, align_bytes=64) for j in range(3)]
+        hq = keep.tile([P, S], U32, name="hq", align_bytes=64)
+        hs = keep.tile([P, S], U8, name="hs", align_bytes=64)
+        o4 = keep.tile([P, 4, T], F32, name="o4", align_bytes=64)
+        ob = keep.tile([P, T, 4], BF16, name="ob", align_bytes=64)
+        oq = keep.tile([P, T], U32, name="oq", align_bytes=64)
+        osc = keep.tile([P, T], U8, name="osc", align_bytes=64)
+
+        nc.vector.memset(y[1][:, S + T :], 0.0)
+        nc.scalar.activation(y[0][:, S + T :], y[1][:, S + T :], SILU)
+        for g in range(2):
+            nc.vector.memset(w2sraw[g][:].bitcast(I32), 0)
+        for t in (2, 3):
+            nc.vector.memset(y[t][:, S + T :], 0.0)
+        make_identity(nc, ident[:])
+
+        def words(src, j):
+            return src[2 * j : 2 * j + 2, 0].rearrange("e p n d -> p e (n d)").bitcast(I32)
+
+        def load_w2s(g, q):
+            n = 4 if g == 0 else 2
+            nc.sync.dma_start(
+                w2sraw[g][32 * q : 32 * q + 4 * n, :].bitcast(I32),
+                w2_scales[4 * g : 4 * g + n, 0, 4 * q : 4 * q + 4, :].bitcast(I32),
+            )
+
+        xr4 = xr.rearrange("(p t) c -> p t c", t=4)
+        out4 = out_0.rearrange("(p t) c -> p t c", t=4)
+
+        nc.sync.dma_start(offs_t[:], offs)
+        nc.sync.dma_start(xw[:].bitcast(I32), x_words[0].rearrange("p t d -> p (t d)").bitcast(I32))
+        for q in range(4):
+            rows = x_scales[0, 4 * q : 4 * q + 4, :].bitcast(I32)
+            nc.sync.dma_start(xs[32 * q : 32 * q + 32, :].bitcast(I32), rows.unsqueeze(0).broadcast_to([8, 4, T // 4]))
+        nc.sync.dma_start(w1[0][:].bitcast(I32), words(w1_words, 0))
+        nc.sync.dma_start(w1[1][:].bitcast(I32), words(w1_words, 1))
+        w1_rows = w1_scales[:, 0].rearrange("e (q r) n -> r q e n", r=4)
+        for r in range(4):
+            nc.sync.dma_start(w1s[r:P:32, :, :].bitcast(I32), w1_rows[r].bitcast(I32))
+        nc.sync.dma_start(w1[2][:].bitcast(I32), words(w1_words, 2))
+        nc.sync.dma_start(w2raw[0][:].bitcast(I32), words(w2_words, 0))
+        for q in range(4):
+            load_w2s(0, q)
+        nc.sync.dma_start(w2raw[1][:].bitcast(I32), words(w2_words, 1))
+        for q in range(4):
+            load_w2s(1, q)
+        nc.sync.dma_start(w2raw[2][:].bitcast(I32), words(w2_words, 2))
+        nc.sync.dma_start(pos1_t[:], pos1)
+        nc.sync.dma_start(y[0][:, S : S + T], xr4[:, 0, :])
+        nc.sync.dma_start(g1[:], gate[0])
+        nc.sync.dma_start(pos2_t[:], pos2)
+        nc.sync.dma_start(g2[:], gate[1])
+        for t in range(1, 4):
+            nc.sync.dma_start(y[t][:, S : S + T], xr4[:, t, :])
+
+        for j in range(3):
+            cut = offs_t[:, 16 * j : 16 * j + 16]
+            nc.vector.tensor_copy(xg[j][:], xw[:].indirect(cut))
+            nc.vector.tensor_copy(xgs[j][:], xs[:].indirect(cut))
+
+        def first_layer(e):
+            j, u = divmod(e, 2)
+            pre = psum.tile([P, H], F32, name="pre")
+            nc.tensor.matmul_mx(
+                out=pre[:],
+                lhsT=xg[j][:, u * C : (u + 1) * C].bitcast(FP8X4),
+                lhsT_scale=xgs[j][:, u * C : (u + 1) * C],
+                rhs=w1[j][:, u, :].bitcast(FP8X4),
+                rhs_scale=w1s[:, e, :],
+                start=True,
+                stop=True,
+            )
+            hb = ring.tile([P, H], BF16, name="hb", align_bytes=64)
+            nc.scalar.activation(
+                hb[:].rearrange("s (u p d) -> s u p d", u=2, d=2), pre[:].rearrange("s (p u d) -> s u p d", u=2, d=2), SILU
+            )
+            return hb
+
+        def turn(e, hb):
+            turned = psum.tile([P, 2, C], F32, name="turned")
+            for u in range(2):
+                nc.tensor.transpose(turned[:, u, :], hb[:].bitcast(F32)[:, u * P : (u + 1) * P], ident[:])
+            hin = ring.tile([P, 4 * C], BF16, name="hin", align_bytes=64)
+            nc.scalar.copy(hin[:].bitcast(F32).rearrange("p (s u) -> p s u", u=2), turned[:].rearrange("p u s -> p s u"))
+            nc.vector.quantize_mx(
+                out=hq[:, e * C : (e + 1) * C].bitcast(FP8X4), scales=hs[:, e * C : (e + 1) * C], in_=hin[:]
+            )
+
+        def deal_words(j):
+            nc.vector.tensor_copy(
+                w2[j][:].bitcast(I32).rearrange("p e (t m) -> p e m t", t=4),
+                w2raw[j][:].bitcast(I32).rearrange("p e (m t) -> p e m t", t=4),
+            )
+
+        def deal_scales(g):
+            nc.vector.tensor_copy(
+                w2s[g][:].rearrange("p (t m) -> p m t", t=4), w2sraw[g][:].rearrange("p (m t) -> p m t", t=4)
+            )
+
+        held = first_layer(0)
+        for e in range(E):
+            nxt = first_layer(e + 1) if e + 1 < E else None
+            turn(e, held)
+            held = nxt
+            if e == 1:
+                deal_words(0)
+            if e == 2:
+                deal_scales(0)
+            if e == 3:
+                deal_words(1)
+            if e == 4:
+                deal_scales(1)
+        deal_words(2)
+
+        accs = [banks.tile([P, 4 * C], F32, name="acc_%d" % b) for b in range(2)]
+
+        def second_layer(t, g):
+            experts = range(4) if g == 0 else range(4, 6)
+            acc = accs[(t + g) % 2]
+            for a, e in enumerate(experts):
+                j, u = divmod(e, 2)
+                nc.tensor.matmul_mx(
+                    out=acc[:, a * C : (a + 1) * C],
+                    lhsT=w2[j][:, u, t * P : (t + 1) * P].bitcast(FP8X4),
+                    lhsT_scale=w2s[g][4 * a : P, t * P : (t + 1) * P],
+                    rhs=hq[:, e * C : (e + 1) * C].bitcast(FP8X4),
+                    rhs_scale=hs[:, e * C : (e + 1) * C],
+                    start=True,
+                    stop=True,
+                )
+            nc.scalar.copy(y[t][:, experts.start * C : experts.stop * C], acc[:, : len(experts) * C])
+
+        for t in range(4):
+            for g in range(2):
+                second_layer(t, g)
+
+        cuts = [(0, 256), (256, 512), (512, T)]
+        steps = [(0, 0, T), (1, 0, T)] + [(t, a, b) for a, b in cuts for t in (2, 3)]
+
+        def fetch(lst, gt, t, a, b, name):
+            got = ring.tile([P, b - a], F32, name=name, align_bytes=64)
+            nc.vector.tensor_tensor(got[:], y[t][:].indirect(lst[:, a // 16 : b // 16]), gt[:, a:b], MULT)
+            return got
+
+        def planes(a, b):
+            nc.scalar.copy(ob[:, a:b, :], o4[:, :, a:b].rearrange("p t c -> p c t"))
+
+        def quantise(a, b):
+            nc.vector.quantize_mx(
+                out=oq[:, a:b].bitcast(FP8X4), scales=osc[:, a:b], in_=ob[:, a:b, :].rearrange("p c t -> p (c t)")
+            )
+            nc.sync.dma_start(
+                out_1[0].rearrange("p c d -> p (c d)").bitcast(I32)[:, a:b], oq[:, a:b].bitcast(I32)
+            )
+
+        first = fetch(pos1_t, g1, *steps[0], "first")
+        for i, (t, a, b) in enumerate(steps):
+            second = fetch(pos2_t, g2, t, a, b, "second")
+            nxt = fetch(pos1_t, g1, *steps[i + 1], "first") if i + 1 < len(steps) else None
+            nc.vector.tensor_tensor(o4[:, t, a:b], first[:], second[:], ADD)
+            nc.sync.dma_start(out4[:, t, a:b], o4[:, t, a:b])
+            first = nxt
+            if t == 3:
+                planes(a, b)
+            if t == 2 and a > 0:
+                quantise(*steps[i - 1][1:])
+        quantise(*steps[-1][1:])
+        for q in range(4):
+            eng = nc.sync if q % 2 == 0 else nc.scalar
+            eng.dma_start(out_2[0, 4 * q : 4 * q + 4, :].bitcast(I32), osc[32 * q : 32 * q + 4, :].bitcast(I32))

@@ -29,8 +29,8 @@ def tile_moe_cpy_mlp_silu_kernel(
         lists = ctx.enter_context(tc.tile_pool(name="lists", bufs=1))
         keep = ctx.enter_context(tc.tile_pool(name="keep", bufs=1))
         ring = ctx.enter_context(tc.tile_pool(name="ring", bufs=3))
-        psum = ctx.enter_context(tc.psum_pool(name="psum", bufs=3))
-        banks = ctx.enter_context(tc.psum_pool(name="banks", bufs=1))
+        psum = ctx.enter_context(tc.psum_pool(name="psum", bufs=1))
+        banks = [psum.tile([P, 4 * P], F32, name="bank_%d" % i) for i in range(8)]
 
         offs_t = lists.tile([P, S // 16], U16, name="offs_t")
         pos1_t = lists.tile([P, T // 16], U16, name="pos1_t")
@@ -40,10 +40,8 @@ def tile_moe_cpy_mlp_silu_kernel(
         xs = keep.tile([P, T], U8, name="xs", align_bytes=64)
         w1 = [keep.tile([P, 2, H], U32, name="w1_%d" % j, align_bytes=64) for j in range(3)]
         w1s = keep.tile([P, E, H], U8, name="w1s", align_bytes=64)
-        w2raw = [keep.tile([P, 2, K], U32, name="w2raw_%d" % j, align_bytes=64) for j in range(3)]
-        w2 = [keep.tile([P, 2, K], U32, name="w2_%d" % j, align_bytes=64) for j in range(3)]
-        w2sraw = [keep.tile([P, K], U8, name="w2sraw_%d" % g, align_bytes=64) for g in range(2)]
-        w2s = [keep.tile([P, K], U8, name="w2s_%d" % g, align_bytes=64) for g in range(2)]
+        w2 = [keep.tile([P, E, n * P], U32, name="w2_%d" % b, align_bytes=64) for b, n in ((0, 1), (1, 1), (2, 2))]
+        w2s = keep.tile([P, E, K], U8, name="w2s", align_bytes=64)
         y = [keep.tile([P, W], F32, name="y_%d" % t, align_bytes=64) for t in range(4)]
         g1 = keep.tile([P, T], F32, name="g1", align_bytes=64)
         g2 = keep.tile([P, T], F32, name="g2", align_bytes=64)
@@ -53,14 +51,12 @@ def tile_moe_cpy_mlp_silu_kernel(
         hq = keep.tile([P, S], U32, name="hq", align_bytes=64)
         hs = keep.tile([P, S], U8, name="hs", align_bytes=64)
         o4 = keep.tile([P, 4, T], F32, name="o4", align_bytes=64)
-        ob = keep.tile([P, T, 4], BF16, name="ob", align_bytes=64)
+        rounded = keep.tile([P, T // P, K], BF16, name="rounded", align_bytes=64)
         oq = keep.tile([P, T], U32, name="oq", align_bytes=64)
         osc = keep.tile([P, T], U8, name="osc", align_bytes=64)
 
         nc.vector.memset(y[1][:, S + T :], 0.0)
         nc.scalar.activation(y[0][:, S + T :], y[1][:, S + T :], SILU)
-        for g in range(2):
-            nc.vector.memset(w2sraw[g][:].bitcast(I32), 0)
         for t in (2, 3):
             nc.vector.memset(y[t][:, S + T :], 0.0)
         make_identity(nc, ident[:])
@@ -68,15 +64,14 @@ def tile_moe_cpy_mlp_silu_kernel(
         def words(src, j):
             return src[2 * j : 2 * j + 2, 0].rearrange("e p n d -> p e (n d)").bitcast(I32)
 
-        def load_w2s(g, q):
-            n = 4 if g == 0 else 2
-            nc.sync.dma_start(
-                w2sraw[g][32 * q : 32 * q + 4 * n, :].bitcast(I32),
-                w2_scales[4 * g : 4 * g + n, 0, 4 * q : 4 * q + 4, :].bitcast(I32),
-            )
+        def load_w2(i, b0, b1):
+            src = w2_words[:, 0, :, b0 * P : b1 * P, :].rearrange("e p n d -> p e (n d)")
+            nc.sync.dma_start(w2[i][:].bitcast(I32), src.bitcast(I32))
 
-        xr4 = xr.rearrange("(p t) c -> p t c", t=4)
-        out4 = out_0.rearrange("(p t) c -> p t c", t=4)
+        def load_xr(b):
+            nc.sync.dma_start(y[b][:, S : S + T], xr[b * P : (b + 1) * P, :])
+
+        out4 = out_0.rearrange("(b p) c -> p b c", p=P)
 
         nc.sync.dma_start(offs_t[:], offs)
         nc.sync.dma_start(xw[:].bitcast(I32), x_words[0].rearrange("p t d -> p (t d)").bitcast(I32))
@@ -89,20 +84,20 @@ def tile_moe_cpy_mlp_silu_kernel(
         for r in range(4):
             nc.sync.dma_start(w1s[r:P:32, :, :].bitcast(I32), w1_rows[r].bitcast(I32))
         nc.sync.dma_start(w1[2][:].bitcast(I32), words(w1_words, 2))
-        nc.sync.dma_start(w2raw[0][:].bitcast(I32), words(w2_words, 0))
-        for q in range(4):
-            load_w2s(0, q)
-        nc.sync.dma_start(w2raw[1][:].bitcast(I32), words(w2_words, 1))
-        for q in range(4):
-            load_w2s(1, q)
-        nc.sync.dma_start(w2raw[2][:].bitcast(I32), words(w2_words, 2))
+        load_w2(0, 0, 1)
         nc.sync.dma_start(pos1_t[:], pos1)
-        nc.sync.dma_start(y[0][:, S : S + T], xr4[:, 0, :])
+        load_xr(0)
+        w2_rows = w2_scales[:, 0].rearrange("e (q r) n -> r q e n", r=4)
+        for r in range(4):
+            nc.sync.dma_start(w2s[r:P:32, :, :].bitcast(I32), w2_rows[r].bitcast(I32))
         nc.sync.dma_start(g1[:], gate[0])
         nc.sync.dma_start(pos2_t[:], pos2)
         nc.sync.dma_start(g2[:], gate[1])
-        for t in range(1, 4):
-            nc.sync.dma_start(y[t][:, S : S + T], xr4[:, t, :])
+        load_w2(1, 1, 2)
+        load_xr(1)
+        load_w2(2, 2, 4)
+        load_xr(2)
+        load_xr(3)
 
         for j in range(3):
             cut = offs_t[:, 16 * j : 16 * j + 16]
@@ -111,7 +106,7 @@ def tile_moe_cpy_mlp_silu_kernel(
 
         def first_layer(e):
             j, u = divmod(e, 2)
-            pre = psum.tile([P, H], F32, name="pre")
+            pre = banks[e % 3]
             nc.tensor.matmul_mx(
                 out=pre[:],
                 lhsT=xg[j][:, u * C : (u + 1) * C].bitcast(FP8X4),
@@ -128,52 +123,35 @@ def tile_moe_cpy_mlp_silu_kernel(
             return hb
 
         def turn(e, hb):
-            turned = psum.tile([P, 2, C], F32, name="turned")
+            turned = banks[3 + e % 3][:, : 2 * C].rearrange("p (u s) -> p u s", u=2)
             for u in range(2):
                 nc.tensor.transpose(turned[:, u, :], hb[:].bitcast(F32)[:, u * P : (u + 1) * P], ident[:])
             hin = ring.tile([P, 4 * C], BF16, name="hin", align_bytes=64)
-            nc.scalar.copy(hin[:].bitcast(F32).rearrange("p (s u) -> p s u", u=2), turned[:].rearrange("p u s -> p s u"))
+            move = nc.vector.tensor_copy if e < 4 else nc.scalar.copy
+            move(hin[:].bitcast(F32).rearrange("p (s u) -> p s u", u=2), turned.rearrange("p u s -> p s u"))
+            return hin
+
+        def quantise_hidden(e, hin):
             nc.vector.quantize_mx(
                 out=hq[:, e * C : (e + 1) * C].bitcast(FP8X4), scales=hs[:, e * C : (e + 1) * C], in_=hin[:]
             )
 
-        def deal_words(j):
-            nc.vector.tensor_copy(
-                w2[j][:].bitcast(I32).rearrange("p e (t m) -> p e m t", t=4),
-                w2raw[j][:].bitcast(I32).rearrange("p e (m t) -> p e m t", t=4),
-            )
-
-        def deal_scales(g):
-            nc.vector.tensor_copy(
-                w2s[g][:].rearrange("p (t m) -> p m t", t=4), w2sraw[g][:].rearrange("p (m t) -> p m t", t=4)
-            )
-
-        held = first_layer(0)
+        active = [first_layer(e) for e in range(2)]
+        hin = turn(0, active[0])
         for e in range(E):
-            nxt = first_layer(e + 1) if e + 1 < E else None
-            turn(e, held)
-            held = nxt
-            if e == 1:
-                deal_words(0)
-            if e == 2:
-                deal_scales(0)
-            if e == 3:
-                deal_words(1)
-            if e == 4:
-                deal_scales(1)
-        deal_words(2)
+            if e + 2 < E:
+                active.append(first_layer(e + 2))
+            nxt = turn(e + 1, active[e + 1]) if e + 1 < E else None
+            quantise_hidden(e, hin)
+            hin = nxt
 
-        accs = [banks.tile([P, 4 * C], F32, name="acc_%d" % b) for b in range(2)]
-
-        def second_layer(t, g):
-            experts = range(4) if g == 0 else range(4, 6)
-            acc = accs[(t + g) % 2]
+        def second_layer(t, experts, acc):
             for a, e in enumerate(experts):
-                j, u = divmod(e, 2)
+                i, part = min(t, 2), max(t - 2, 0)
                 nc.tensor.matmul_mx(
                     out=acc[:, a * C : (a + 1) * C],
-                    lhsT=w2[j][:, u, t * P : (t + 1) * P].bitcast(FP8X4),
-                    lhsT_scale=w2s[g][4 * a : P, t * P : (t + 1) * P],
+                    lhsT=w2[i][:, e, part * P : (part + 1) * P].bitcast(FP8X4),
+                    lhsT_scale=w2s[:, e, t * P : (t + 1) * P],
                     rhs=hq[:, e * C : (e + 1) * C].bitcast(FP8X4),
                     rhs_scale=hs[:, e * C : (e + 1) * C],
                     start=True,
@@ -181,41 +159,100 @@ def tile_moe_cpy_mlp_silu_kernel(
                 )
             nc.scalar.copy(y[t][:, experts.start * C : experts.stop * C], acc[:, : len(experts) * C])
 
-        for t in range(4):
-            for g in range(2):
-                second_layer(t, g)
+        early, late = range(4), range(4, E)
+        second_layer(0, early, banks[6])
+        second_layer(0, late, banks[0])
+        second_layer(1, late, banks[7])
+        second_layer(1, early, banks[0])
+        second_layer(2, late, banks[2])
+        second_layer(2, early, banks[7])
+        second_layer(3, early, banks[0])
+        second_layer(3, late, banks[3])
 
         cuts = [(0, 256), (256, 512), (512, T)]
-        steps = [(0, 0, T), (1, 0, T)] + [(t, a, b) for a, b in cuts for t in (2, 3)]
+        NB = T // P
 
-        def fetch(lst, gt, t, a, b, name):
-            got = ring.tile([P, b - a], F32, name=name, align_bytes=64)
-            nc.vector.tensor_tensor(got[:], y[t][:].indirect(lst[:, a // 16 : b // 16]), gt[:, a:b], MULT)
+        def fetch(lst, gt, b, lo, hi, name):
+            got = ring.tile([P, hi - lo], F32, name=name, align_bytes=64)
+            nc.vector.tensor_tensor(got[:], y[b][:].indirect(lst[:, lo // 16 : hi // 16]), gt[:, lo:hi], MULT)
             return got
 
-        def planes(a, b):
-            nc.scalar.copy(ob[:, a:b, :], o4[:, :, a:b].rearrange("p t c -> p c t"))
-
-        def quantise(a, b):
-            nc.vector.quantize_mx(
-                out=oq[:, a:b].bitcast(FP8X4), scales=osc[:, a:b], in_=ob[:, a:b, :].rearrange("p c t -> p (c t)")
-            )
-            nc.sync.dma_start(
-                out_1[0].rearrange("p c d -> p (c d)").bitcast(I32)[:, a:b], oq[:, a:b].bitcast(I32)
+        def round_turned(bank, cs, b0, b1):
+            dst = rounded[:, cs.start : cs.stop, :].rearrange("s c (u p d) -> s c u p d", u=2, d=2)
+            nc.scalar.copy(
+                dst[:, :, :, 32 * b0 : 32 * b1, :], bank.rearrange("s (c p u d) -> s c u p d", c=len(cs), u=2, d=2)
             )
 
+        def sum_turned(b, pair):
+            terms = [fetch(pos1_t, g1, b, 0, T, "first"), fetch(pos2_t, g2, b, 0, T, "second")]
+            summed = keep.tile([P, T], F32, name="summed_%d" % b, align_bytes=64)
+            for cs, whole in zip((range(0, 4), range(4, NB)), pair):
+                bank = whole[:, : len(cs) * P]
+                for c in cs:
+                    for r in range(2):
+                        nc.tensor.matmul(
+                            bank[:, (c - cs.start) * P : (c - cs.start + 1) * P],
+                            terms[r][:, c * P : (c + 1) * P],
+                            ident[:],
+                            start=(r == 0),
+                            stop=(r == 1),
+                            is_transpose=True,
+                        )
+                round_turned(bank, cs, b, b + 1)
+            for cs, whole in zip((range(0, 4), range(4, NB)), pair):
+                nc.scalar.copy(summed[:, cs.start * P : cs.stop * P], whole[:, : len(cs) * P])
+            return summed
+
+        def turn_back(b, summed, pair):
+            for cs, whole in zip((range(0, 4), range(4, NB)), pair):
+                for c in cs:
+                    at = (c - cs.start) * P
+                    nc.tensor.transpose(whole[:, at : at + P], summed[:, c * P : (c + 1) * P], ident[:])
+                nc.scalar.copy(o4[:, b, cs.start * P : cs.stop * P], whole[:, : len(cs) * P])
+            nc.sync.dma_start(out4[:, b, :], o4[:, b, :])
+
+        def round_cut(lo, hi):
+            cs = range(lo // P, hi // P)
+            bank = banks[0][:, : 2 * (hi - lo)]
+            for a, c in enumerate(cs):
+                for b in (2, 3):
+                    at = (2 * a + b - 2) * P
+                    nc.tensor.transpose(bank[:, at : at + P], o4[:, b, c * P : (c + 1) * P], ident[:])
+            round_turned(bank, cs, 2, 4)
+
+        def words_cut(lo, hi):
+            cs = range(lo // P, hi // P)
+            back = banks[2 + cs.start // 2][:, : 2 * (hi - lo)]
+            back = back.rearrange("p (c u s) -> p c u s", u=2, s=P)
+            for a, c in enumerate(cs):
+                for u in range(2):
+                    nc.tensor.transpose(back[:, a, u, :], rounded[:, c, :].bitcast(F32)[:, u * P : (u + 1) * P], ident[:])
+            ob = ring.tile([P, 4 * (hi - lo)], BF16, name="ob", align_bytes=64)
+            move = nc.scalar.copy if lo == 0 else nc.vector.tensor_copy
+            move(
+                ob[:].bitcast(F32).rearrange("p (c s u) -> p c s u", c=len(cs), u=2),
+                back.rearrange("p c u s -> p c s u"),
+            )
+            return ob
+
+        turn_back(0, sum_turned(0, (banks[2], banks[3])), banks[4:6])
+        turn_back(1, sum_turned(1, (banks[3], banks[0])), (banks[6], banks[1]))
+
+        def quantise(lo, hi, ob):
+            nc.vector.quantize_mx(out=oq[:, lo:hi].bitcast(FP8X4), scales=osc[:, lo:hi], in_=ob[:])
+            nc.sync.dma_start(out_1[0].rearrange("p c d -> p (c d)").bitcast(I32)[:, lo:hi], oq[:, lo:hi].bitcast(I32))
+
+        steps = [(b, lo, hi) for lo, hi in cuts for b in (2, 3)]
         first = fetch(pos1_t, g1, *steps[0], "first")
-        for i, (t, a, b) in enumerate(steps):
-            second = fetch(pos2_t, g2, t, a, b, "second")
+        for i, (b, lo, hi) in enumerate(steps):
+            second = fetch(pos2_t, g2, b, lo, hi, "second")
             nxt = fetch(pos1_t, g1, *steps[i + 1], "first") if i + 1 < len(steps) else None
-            nc.vector.tensor_tensor(o4[:, t, a:b], first[:], second[:], ADD)
-            nc.sync.dma_start(out4[:, t, a:b], o4[:, t, a:b])
+            nc.vector.tensor_tensor(o4[:, b, lo:hi], first[:], second[:], ADD)
+            nc.sync.dma_start(out4[:, b, lo:hi], o4[:, b, lo:hi])
             first = nxt
-            if t == 3:
-                planes(a, b)
-            if t == 2 and a > 0:
-                quantise(*steps[i - 1][1:])
-        quantise(*steps[-1][1:])
+            if b == 3:
+                round_cut(lo, hi)
+                quantise(lo, hi, words_cut(lo, hi))
         for q in range(4):
             eng = nc.sync if q % 2 == 0 else nc.scalar
             eng.dma_start(out_2[0, 4 * q : 4 * q + 4, :].bitcast(I32), osc[32 * q : 32 * q + 4, :].bitcast(I32))

from contextlib import ExitStack

import concourse.mybir as mybir
from concourse.masks import make_identity

K, T, E, C, H, PAD = 512, 640, 6, 128, 512, 64
S = E * C
W = S + T + PAD
FLOPS = 2 * 2 * S * K * H

F32 = mybir.dt.float32
BF16 = mybir.dt.bfloat16
I32 = mybir.dt.int32
U32 = mybir.dt.uint32
U16 = mybir.dt.uint16
U8 = mybir.dt.uint8
FP8X4 = mybir.dt.float8_e4m3fn_x4
MULT = mybir.AluOpType.mult
ADD = mybir.AluOpType.add
SILU = mybir.ActivationFunctionType.Silu
P = 128


def tile_moe_cpy_mlp_silu_kernel(
    tc, x_words, x_scales, xr, w1_words, w1_scales, w2_words, w2_scales, gate, offs, pos1, pos2, out_0, out_1, out_2
):
    nc = tc.nc
    with ExitStack() as ctx:
        lists = ctx.enter_context(tc.tile_pool(name="lists", bufs=1))
        keep = ctx.enter_context(tc.tile_pool(name="keep", bufs=1))
        ring = ctx.enter_context(tc.tile_pool(name="ring", bufs=3))
        psum = ctx.enter_context(tc.psum_pool(name="psum", bufs=1))
        banks = [psum.tile([P, 4 * P], F32, name="bank_%d" % i) for i in range(8)]

        offs_t = lists.tile([P, S // 16], U16, name="offs_t")
        pos1_t = lists.tile([P, T // 16], U16, name="pos1_t")
        pos2_t = lists.tile([P, T // 16], U16, name="pos2_t")

        xw = keep.tile([P, T], U32, name="xw", align_bytes=64)
        xs = keep.tile([P, T], U8, name="xs", align_bytes=64)
        w1 = [keep.tile([P, 2, H], U32, name="w1_%d" % j, align_bytes=64) for j in range(3)]
        w1s = keep.tile([P, E, H], U8, name="w1s", align_bytes=64)
        w2 = [keep.tile([P, E, n * P], U32, name="w2_%d" % b, align_bytes=64) for b, n in ((0, 1), (1, 1), (2, 2))]
        w2s = keep.tile([P, E, K], U8, name="w2s", align_bytes=64)
        y = [keep.tile([P, W], F32, name="y_%d" % t, align_bytes=64) for t in range(4)]
        g1 = keep.tile([P, T], F32, name="g1", align_bytes=64)
        g2 = keep.tile([P, T], F32, name="g2", align_bytes=64)
        ident = keep.tile([P, P], F32, name="ident", align_bytes=64)
        xg = [keep.tile([P, 2 * C], U32, name="xg_%d" % j, align_bytes=64) for j in range(3)]
        xgs = [keep.tile([P, 2 * C], U8, name="xgs_%d" % j, align_bytes=64) for j in range(3)]
        hq = keep.tile([P, S], U32, name="hq", align_bytes=64)
        hs = keep.tile([P, S], U8, name="hs", align_bytes=64)
        o4 = keep.tile([P, 4, T], F32, name="o4", align_bytes=64)
        rounded = keep.tile([P, T // P, K], BF16, name="rounded", align_bytes=64)
        oq = keep.tile([P, T], U32, name="oq", align_bytes=64)
        osc = keep.tile([P, T], U8, name="osc", align_bytes=64)

        nc.vector.memset(y[1][:, S + T :], 0.0)
        nc.scalar.activation(y[0][:, S + T :], y[1][:, S + T :], SILU)
        for t in (2, 3):
            nc.vector.memset(y[t][:, S + T :], 0.0)
        make_identity(nc, ident[:])

        def words(src, j):
            return src[2 * j : 2 * j + 2, 0].rearrange("e p n d -> p e (n d)").bitcast(I32)

        def load_w2(i, b0, b1):
            src = w2_words[:, 0, :, b0 * P : b1 * P, :].rearrange("e p n d -> p e (n d)")
            nc.sync.dma_start(w2[i][:].bitcast(I32), src.bitcast(I32))

        def load_xr(b):
            nc.sync.dma_start(y[b][:, S : S + T], xr[b * P : (b + 1) * P, :])

        out4 = out_0.rearrange("(b p) c -> p b c", p=P)

        nc.sync.dma_start(offs_t[:], offs)
        nc.sync.dma_start(xw[:].bitcast(I32), x_words[0].rearrange("p t d -> p (t d)").bitcast(I32))
        for q in range(4):
            rows = x_scales[0, 4 * q : 4 * q + 4, :].bitcast(I32)
            nc.sync.dma_start(xs[32 * q : 32 * q + 32, :].bitcast(I32), rows.unsqueeze(0).broadcast_to([8, 4, T // 4]))
        nc.sync.dma_start(w1[0][:].bitcast(I32), words(w1_words, 0))
        nc.sync.dma_start(w1[1][:].bitcast(I32), words(w1_words, 1))
        w1_rows = w1_scales[:, 0].rearrange("e (q r) n -> r q e n", r=4)
        for r in range(4):
            nc.sync.dma_start(w1s[r:P:32, :, :].bitcast(I32), w1_rows[r].bitcast(I32))
        nc.sync.dma_start(w1[2][:].bitcast(I32), words(w1_words, 2))
        load_w2(0, 0, 1)
        nc.sync.dma_start(pos1_t[:], pos1)
        load_xr(0)
        w2_rows = w2_scales[:, 0].rearrange("e (q r) n -> r q e n", r=4)
        for r in range(4):
            nc.sync.dma_start(w2s[r:P:32, :, :].bitcast(I32), w2_rows[r].bitcast(I32))
        nc.sync.dma_start(g1[:], gate[0])
        nc.sync.dma_start(pos2_t[:], pos2)
        nc.sync.dma_start(g2[:], gate[1])
        load_w2(1, 1, 2)
        load_xr(1)
        load_w2(2, 2, 4)
        load_xr(2)
        load_xr(3)

        for j in range(3):
            cut = offs_t[:, 16 * j : 16 * j + 16]
            nc.vector.tensor_copy(xg[j][:], xw[:].indirect(cut))
            nc.vector.tensor_copy(xgs[j][:], xs[:].indirect(cut))

        def first_layer(e):
            j, u = divmod(e, 2)
            pre = banks[e % 3]
            nc.tensor.matmul_mx(
                out=pre[:],
                lhsT=xg[j][:, u * C : (u + 1) * C].bitcast(FP8X4),
                lhsT_scale=xgs[j][:, u * C : (u + 1) * C],
                rhs=w1[j][:, u, :].bitcast(FP8X4),
                rhs_scale=w1s[:, e, :],
                start=True,
                stop=True,
            )
            hb = ring.tile([P, H], BF16, name="hb", align_bytes=64)
            nc.scalar.activation(
                hb[:].rearrange("s (u p d) -> s u p d", u=2, d=2), pre[:].rearrange("s (p u d) -> s u p d", u=2, d=2), SILU
            )
            return hb

        def turn(e, hb):
            turned = banks[3 + e % 3][:, : 2 * C].rearrange("p (u s) -> p u s", u=2)
            for u in range(2):
                nc.tensor.transpose(turned[:, u, :], hb[:].bitcast(F32)[:, u * P : (u + 1) * P], ident[:])
            hin = ring.tile([P, 4 * C], BF16, name="hin", align_bytes=64)
            move = nc.vector.tensor_copy if e < 4 else nc.scalar.copy
            move(hin[:].bitcast(F32).rearrange("p (s u) -> p s u", u=2), turned.rearrange("p u s -> p s u"))
            return hin

        def quantise_hidden(e, hin):
            nc.vector.quantize_mx(
                out=hq[:, e * C : (e + 1) * C].bitcast(FP8X4), scales=hs[:, e * C : (e + 1) * C], in_=hin[:]
            )

        active = [first_layer(e) for e in range(2)]
        hin = turn(0, active[0])
        for e in range(E):
            if e + 2 < E:
                active.append(first_layer(e + 2))
            nxt = turn(e + 1, active[e + 1]) if e + 1 < E else None
            quantise_hidden(e, hin)
            hin = nxt

        def second_layer(t, experts, acc):
            for a, e in enumerate(experts):
                i, part = min(t, 2), max(t - 2, 0)
                nc.tensor.matmul_mx(
                    out=acc[:, a * C : (a + 1) * C],
                    lhsT=w2[i][:, e, part * P : (part + 1) * P].bitcast(FP8X4),
                    lhsT_scale=w2s[:, e, t * P : (t + 1) * P],
                    rhs=hq[:, e * C : (e + 1) * C].bitcast(FP8X4),
                    rhs_scale=hs[:, e * C : (e + 1) * C],
                    start=True,
                    stop=True,
                )
            nc.scalar.copy(y[t][:, experts.start * C : experts.stop * C], acc[:, : len(experts) * C])

        early, late = range(4), range(4, E)
        second_layer(0, early, banks[6])
        second_layer(0, late, banks[0])
        second_layer(1, late, banks[7])
        second_layer(1, early, banks[0])
        second_layer(2, late, banks[2])
        second_layer(2, early, banks[7])
        second_layer(3, early, banks[0])
        second_layer(3, late, banks[3])

        cuts = [(0, 256), (256, 512), (512, T)]
        NB = T // P

        def fetch(lst, gt, b, lo, hi, name):
            got = ring.tile([P, hi - lo], F32, name=name, align_bytes=64)
            nc.vector.tensor_tensor(got[:], y[b][:].indirect(lst[:, lo // 16 : hi // 16]), gt[:, lo:hi], MULT)
            return got

        def round_turned(bank, cs, b0, b1):
            dst = rounded[:, cs.start : cs.stop, :].rearrange("s c (u p d) -> s c u p d", u=2, d=2)
            nc.scalar.copy(
                dst[:, :, :, 32 * b0 : 32 * b1, :], bank.rearrange("s (c p u d) -> s c u p d", c=len(cs), u=2, d=2)
            )

        def sum_turned(b, pair):
            terms = [fetch(pos1_t, g1, b, 0, T, "first"), fetch(pos2_t, g2, b, 0, T, "second")]
            summed = keep.tile([P, T], F32, name="summed_%d" % b, align_bytes=64)
            for cs, whole in zip((range(0, 4), range(4, NB)), pair):
                bank = whole[:, : len(cs) * P]
                for c in cs:
                    for r in range(2):
                        nc.tensor.matmul(
                            bank[:, (c - cs.start) * P : (c - cs.start + 1) * P],
                            terms[r][:, c * P : (c + 1) * P],
                            ident[:],
                            start=(r == 0),
                            stop=(r == 1),
                            is_transpose=True,
                        )
                round_turned(bank, cs, b, b + 1)
            for cs, whole in zip((range(0, 4), range(4, NB)), pair):
                nc.scalar.copy(summed[:, cs.start * P : cs.stop * P], whole[:, : len(cs) * P])
            return summed

        def turn_back(b, summed, pair):
            for cs, whole in zip((range(0, 4), range(4, NB)), pair):
                for c in cs:
                    at = (c - cs.start) * P
                    nc.tensor.transpose(whole[:, at : at + P], summed[:, c * P : (c + 1) * P], ident[:])
                nc.scalar.copy(o4[:, b, cs.start * P : cs.stop * P], whole[:, : len(cs) * P])
            nc.sync.dma_start(out4[:, b, :], o4[:, b, :])

        def round_cut(lo, hi):
            cs = range(lo // P, hi // P)
            bank = banks[0][:, : 2 * (hi - lo)]
            for a, c in enumerate(cs):
                for b in (2, 3):
                    at = (2 * a + b - 2) * P
                    nc.tensor.transpose(bank[:, at : at + P], o4[:, b, c * P : (c + 1) * P], ident[:])
            round_turned(bank, cs, 2, 4)

        def words_cut(lo, hi):
            cs = range(lo // P, hi // P)
            back = banks[2 + cs.start // 2][:, : 2 * (hi - lo)]
            back = back.rearrange("p (c u s) -> p c u s", u=2, s=P)
            for a, c in enumerate(cs):
                for u in range(2):
                    nc.tensor.transpose(back[:, a, u, :], rounded[:, c, :].bitcast(F32)[:, u * P : (u + 1) * P], ident[:])
            ob = ring.tile([P, 4 * (hi - lo)], BF16, name="ob", align_bytes=64)
            move = nc.scalar.copy if lo == 0 else nc.vector.tensor_copy
            move(
                ob[:].bitcast(F32).rearrange("p (c s u) -> p c s u", c=len(cs), u=2),
                back.rearrange("p c u s -> p c s u"),
            )
            return ob

        turn_back(0, sum_turned(0, (banks[2], banks[3])), banks[4:6])
        turn_back(1, sum_turned(1, (banks[3], banks[0])), (banks[6], banks[1]))

        def quantise(lo, hi, ob):
            nc.vector.quantize_mx(out=oq[:, lo:hi].bitcast(FP8X4), scales=osc[:, lo:hi], in_=ob[:])
            nc.sync.dma_start(out_1[0].rearrange("p c d -> p (c d)").bitcast(I32)[:, lo:hi], oq[:, lo:hi].bitcast(I32))

        steps = [(b, lo, hi) for lo, hi in cuts for b in (2, 3)]
        first = fetch(pos1_t, g1, *steps[0], "first")
        for i, (b, lo, hi) in enumerate(steps):
            second = fetch(pos2_t, g2, b, lo, hi, "second")
            nxt = fetch(pos1_t, g1, *steps[i + 1], "first") if i + 1 < len(steps) else None
            nc.vector.tensor_tensor(o4[:, b, lo:hi], first[:], second[:], ADD)
            nc.sync.dma_start(out4[:, b, lo:hi], o4[:, b, lo:hi])
            first = nxt
            if b == 3:
                round_cut(lo, hi)
                quantise(lo, hi, words_cut(lo, hi))
        for q in range(4):
            eng = nc.sync if q % 2 == 0 else nc.scalar
            eng.dma_start(out_2[0, 4 * q : 4 * q + 4, :].bitcast(I32), osc[32 * q : 32 * q + 4, :].bitcast(I32))
